import numpy as np, ml_dtypes
CORES = [65,73,81,89,97,105,113,121]
N = 8
C = 32
def setup_inputs(rng):
    x = rng.standard_normal((N, 128, C), dtype=np.float32) * (0.25 + np.abs(rng.standard_normal((N, 1, C), dtype=np.float32)))
    return {"x": x.astype(ml_dtypes.bfloat16)}
def setup_inputs_big(rng):
    d = setup_inputs(rng)
    for k in ("x",): d[k] = (d[k].astype(np.float32) * 1048576.0).astype(d[k].dtype)
    return d
def setup_inputs_small(rng):
    d = setup_inputs(rng)
    for k in ("x",): d[k] = (d[k].astype(np.float32) * (1 / 1048576.0)).astype(d[k].dtype)
    return d
def setup_inputs_apart(rng):
    d = setup_inputs(rng)
    f = (10.0 ** rng.permutation(np.linspace(-1.5, 1.5, N))).astype(np.float32).reshape(N, 1, 1)
    for k in ("x",): d[k] = (d[k].astype(np.float32) * f).astype(d[k].dtype)
    return d
def setup_inputs_mixed(rng):
    d = setup_inputs(rng)
    f = (10.0 ** rng.uniform(-3, 3, (N, 1, C))).astype(np.float32); shape = rng.integers(3, size=(N, 1, C))
    for k in ("x",):
        x = d[k].astype(np.float32)
        m = x.mean(axis=1, keepdims=True); level = m + np.sign(x - m) * np.abs(x - m).mean(axis=1, keepdims=True) * rng.uniform(0.9, 1.1, x.shape).astype(np.float32)
        other = x * np.where(rng.random(x.shape) < 0.016, 100.0, 1.0).astype(np.float32)
        d[k] = (np.where(shape == 1, level, np.where(shape == 2, other, x)) * f).astype(d[k].dtype)
    return d
def reference(x):
    X = x.astype(np.float64); U = X / np.sqrt((X ** 2).sum(axis=1, keepdims=True))
    y = np.full((N, C, N * C), np.nan)
    for r in range(N):
        for s in range(N):
            if s != r: y[r][:, C * s:C * s + C] = U[r].T @ U[s]
    return {"y": y.astype(ml_dtypes.bfloat16)}

@@ -1,0 +1,165 @@
+from concourse.bass import DstId, RemoteDMATransfer
+from concourse.mybir import AluOpType, ActivationFunctionType
+
+P, N, C = 128, 8, 32
+H = N // 2
+W = H * C
+K_HOP1 = 4
+K_HOP2 = 8
+K_NEAR = 8
+
+_BF, _F = "bfloat16", "float32"
+SCRATCH = {
+    "xd": ("dram", [P, C], _BF),
+    "rd": ("dram", [P, C], _BF),
+    "xa": ("sbuf", [P, W], _BF),
+    "xb": ("sbuf", [P, W], _BF),
+    "sqo": ("sbuf", [P, C], _BF),
+    "sqa": ("sbuf", [P, W], _BF),
+    "sqb": ("sbuf", [P, W], _BF),
+    "one": ("sbuf", [P, 8], _BF),
+    "onem": ("sbuf", [P, P], _BF),
+    "ident": ("sbuf", [P, P], _BF),
+    "ro": ("sbuf", [P, 4], _F),
+    "inv": ("sbuf", [P, 4], _F),
+    "ra": ("sbuf", [P, 4], _F),
+    "rb": ("sbuf", [P, 4], _F),
+    "da": ("sbuf", [P, P], _BF),
+    "db": ("sbuf", [P, P], _BF),
+    "za": ("sbuf", [P, C], _BF),
+    "zb": ("sbuf", [P, C], _BF),
+    "ysb": ("sbuf", [P, H, 2, C], _BF),
+    "pso": ("psum", [P, 512], _F),
+    "pza": ("psum", [P, 512], _F),
+    "psa": ("psum", [P, 512], _F),
+    "pya": ("psum", [P, 512], _F),
+    "pzb": ("psum", [P, 512], _F),
+    "psb": ("psum", [P, 512], _F),
+    "pyb": ("psum", [P, 512], _F),
+}
+SEMAPHORES = ["ldd", "ldx", "one", "onem", "idm", "rarr", "arra", "arrb", "snd", "st",
+              "sqo", "pso", "ro", "inv"] + [n + t for t in "ab" for n in ("sq", "pz", "ps", "z", "r", "d", "py", "o")]
+
+
+def _plan(T, topo, r):
+    cores = list(T.cores)
+    ch = topo.chip(cores[r])
+    near = [s for s in range(len(cores))
+            if topo.chip(cores[s]) == ch or topo.same_plane(topo.chip(cores[s]), ch)]
+    far = [s for s in range(len(cores)) if s not in near]
+    owners = [c for c in range(topo.CHIPS * topo.CORES_PER_CHIP)
+              if topo.chip(c) == ch and c not in cores and all(topo.may_write(c, cores[d]) for d in far)]
+    owners = owners[:len(far)]
+    return near, far, {c: far[i::len(owners)] for i, c in enumerate(owners)}
+
+
+def _pick(mask, k, avoid=0):
+    bits = [b for b in range(mask.bit_length()) if (mask >> b) & 1 and not (avoid >> b) & 1]
+    if len(bits) < k:
+        bits = [b for b in range(mask.bit_length()) if (mask >> b) & 1]
+    return sum(1 << b for b in bits[:k])
+
+
+def _common_mask(topo, src, dsts):
+    m = topo.mask(src, dsts[0])
+    for d in dsts[1:]:
+        m &= topo.mask(src, d)
+    return m
+
+
+def _send(g, topo, src_ap, dst_ap, dsts, mask, remote_sem, local_sem):
+    ids = [DstId(rid=topo.addr(d)[0], pnc=topo.addr(d)[1]) for d in dsts]
+    g.remote_dma_fused([RemoteDMATransfer(dst_ids=ids, dma_engine_mask=mask, remote_sem=remote_sem,
+                                          srcs=[src_ap], dsts=[dst_ap for _ in dsts])], local_sem=local_sem)
+
+
+def _tile(g, T, t, arrived, own, col):
+    S = T.sem
+    X, SQ, Z, R, D = T["x" + t], T["sq" + t], T["z" + t], T["r" + t], T["d" + t]
+    PZ, PS, PY = T["pz" + t], T["ps" + t], T["py" + t]
+    for q in (g.scalar, g.tensor):
+        for sem, v in arrived:
+            q.wait_ge(sem, v)
+    g.scalar.activation(SQ[:], X[:], ActivationFunctionType.Square).then_inc(S["sq" + t], 1)
+    g.tensor.matmul(PZ[:, 0:C], X[:], own, True, True).then_inc(S["pz" + t], 1)
+    g.tensor.wait_ge(S["sq" + t], 1)
+    g.tensor.matmul(PS[:, 0:1], SQ[:], T.one[:, 0:1], True, True).then_inc(S["ps" + t], 1)
+    g.vector.wait_ge(S["pz" + t], 1)
+    g.vector.tensor_copy(Z[:], PZ[:, 0:C]).then_inc(S["z" + t], 1)
+    g.vector.wait_ge(S["ps" + t], 1)
+    g.vector.reciprocal(R[:, 0:1], PS[:, 0:1]).then_inc(S["r" + t], 1)
+    g.scalar.wait_ge(S["r" + t], 1)
+    g.scalar.wait_ge(S.idm, 1)
+    g.scalar.activation(D[:], T.ident[:], ActivationFunctionType.Sqrt, scale=R[:, 0:1]).then_inc(S["d" + t], 1)
+    g.tensor.wait_ge(S["z" + t], 1)
+    g.tensor.wait_ge(S["d" + t], 1)
+    g.tensor.matmul(PY[0:C, 0:W], Z[:], D[:], True, True).then_inc(S["py" + t], 1)
+    g.vector.wait_ge(S["py" + t], 1)
+    g.vector.wait_ge(S.inv, 1)
+    g.vector.tensor_scalar(T.ysb[0:C, :, col, :], PY[0:C, 0:W], T.inv[0:C, 0:1], None,
+                           AluOpType.mult).then_inc(S["o" + t], 1)
+
+
+def _owner_program(g, core, T, topo):
+    cores = list(T.cores)
+    S = T.sem
+    for r in range(len(cores)):
+        if topo.chip(cores[r]) != topo.chip(core):
+            continue
+        near, far, jobs = _plan(T, topo, r)
+        if core not in jobs:
+            continue
+        slot = near.index(r)
+        dsts = [cores[d] for d in jobs[core]]
+        mask = _pick(_common_mask(topo, core, dsts), K_HOP2)
+        g.wait_ge(S.rarr, K_HOP1)
+        _send(g, topo, T.rd[:], T.xb[:, slot * C:(slot + 1) * C], dsts, mask, S.arrb, S.snd)
+        g.wait_ge(S.snd, K_HOP2)
+
+
+def rank_program(g, core, T, topo):
+    r = T.rank_of(core)
+    if r is None:
+        _owner_program(g, core, T, topo)
+        return
+    S = T.sem
+    cores = list(T.cores)
+    near, far, jobs = _plan(T, topo, r)
+    assert near == list(range(near[0], N, 2)) and far == list(range(far[0], N, 2))
+    slot = near.index(r)
+    own = T.xa[:, slot * C:(slot + 1) * C]
+    peers = [cores[s] for s in near if s != r]
+    owners = list(jobs)
+
+    g.sync.dma_start(T.xd[:], T.x[:]).then_inc(S.ldd, 16)
+    g.scalar.dma_start(own, T.x[:]).then_inc(S.ldx, 16)
+
+    g.vector.memset(T.onem[:], 1.0).then_inc(S.onem, 1)
+    g.vector.memset(T.one[:], 1.0).then_inc(S.one, 1)
+    g.wait_ge(S.onem, 1)
+    g.affine_select(T.ident[:], T.onem[:], [[-1, P]], AluOpType.is_equal, 0.0, 0, 1).then_inc(S.idm, 1)
+
+    m_near = _pick(_common_mask(topo, core, peers), K_NEAR)
+    m_hop1 = _pick(_common_mask(topo, core, owners), K_HOP1, avoid=m_near)
+    g.wait_ge(S.ldd, 16)
+    _send(g, topo, T.xd[:], T.rd[:], owners, m_hop1, S.rarr, S.snd)
+    _send(g, topo, T.xd[:], own, peers, m_near, S.arra, S.snd)
+
+    g.scalar.wait_ge(S.ldx, 16)
+    g.scalar.activation(T.sqo[:], own, ActivationFunctionType.Square).then_inc(S.sqo, 1)
+    g.tensor.wait_ge(S.sqo, 1)
+    g.tensor.wait_ge(S.one, 1)
+    g.tensor.matmul(T.pso[0:C, 0:1], T.sqo[:], T.one[:, 0:1], True, True).then_inc(S.pso, 1)
+    g.vector.wait_ge(S.pso, 1)
+    g.vector.reciprocal(T.ro[0:C, 0:1], T.pso[0:C, 0:1]).then_inc(S.ro, 1)
+    g.scalar.wait_ge(S.ro, 1)
+    g.scalar.activation(T.inv[0:C, 0:1], T.ro[0:C, 0:1], ActivationFunctionType.Sqrt).then_inc(S.inv, 1)
+
+    _tile(g, T, "a", [(S.ldx, 16), (S.arra, K_NEAR * len(peers))], own, near[0])
+    _tile(g, T, "b", [(S.arrb, K_HOP2 * len(far))], own, far[0])
+
+    g.sync.wait_ge(S.oa, 1)
+    g.sync.wait_ge(S.ob, 1)
+    g.sync.dma_start(T.y[:], T.ysb[0:C]).then_inc(S.st, 16)
+    g.sync.wait_ge(S.st, 16)
+    g.wait_ge(S.snd, K_HOP1 + K_NEAR)

@@ -7,38 +7,43 @@ W = H * C
 K_HOP1 = 4
 K_HOP2 = 8
 K_NEAR = 8
+K_INFO = 16
 
 _BF, _F = "bfloat16", "float32"
 SCRATCH = {
     "xd": ("dram", [P, C], _BF),
     "rd": ("dram", [P, C], _BF),
+    "rd2": ("dram", [P, C], _BF),
     "xa": ("sbuf", [P, W], _BF),
     "xb": ("sbuf", [P, W], _BF),
-    "sqo": ("sbuf", [P, C], _BF),
+    "drb": ("sbuf", [P, W], _BF),
+    "drs": ("sbuf", [P, C], _BF),
+    "sqf": ("sbuf", [P, W], _BF),
     "sqa": ("sbuf", [P, W], _BF),
-    "sqb": ("sbuf", [P, W], _BF),
     "one": ("sbuf", [P, 8], _BF),
     "onem": ("sbuf", [P, P], _BF),
     "ident": ("sbuf", [P, P], _BF),
+    "rf": ("sbuf", [P, 4], _F),
     "ro": ("sbuf", [P, 4], _F),
     "inv": ("sbuf", [P, 4], _F),
     "ra": ("sbuf", [P, 4], _F),
-    "rb": ("sbuf", [P, 4], _F),
     "da": ("sbuf", [P, P], _BF),
     "db": ("sbuf", [P, P], _BF),
     "za": ("sbuf", [P, C], _BF),
     "zb": ("sbuf", [P, C], _BF),
     "ysb": ("sbuf", [P, H, 2, C], _BF),
+    "psf": ("psum", [P, 512], _F),
     "pso": ("psum", [P, 512], _F),
     "pza": ("psum", [P, 512], _F),
     "psa": ("psum", [P, 512], _F),
     "pya": ("psum", [P, 512], _F),
     "pzb": ("psum", [P, 512], _F),
-    "psb": ("psum", [P, 512], _F),
     "pyb": ("psum", [P, 512], _F),
 }
-SEMAPHORES = ["ldd", "ldx", "one", "onem", "idm", "rarr", "arra", "arrb", "snd", "st",
-              "sqo", "pso", "ro", "inv"] + [n + t for t in "ab" for n in ("sq", "pz", "ps", "z", "r", "d", "py", "o")]
+SEMAPHORES = ["ldd", "ldx", "one", "onem", "sqm", "idm", "rarr", "rarr2", "arra", "arrb", "arrd", "snd", "st",
+              "sqo", "psf", "rf", "drs", "pso", "ro", "inv",
+              "sqa", "pza", "psa", "za", "ra", "da", "pya", "oa", "pzb", "zb", "db", "pyb", "ob"]
+_ACT = ActivationFunctionType
 
 
 def _plan(T, topo, r):
@@ -50,14 +55,16 @@ def _plan(T, topo, r):
     owners = [c for c in range(topo.CHIPS * topo.CORES_PER_CHIP)
               if topo.chip(c) == ch and c not in cores and all(topo.may_write(c, cores[d]) for d in far)]
     owners = owners[:len(far)]
-    return near, far, {c: far[i::len(owners)] for i, c in enumerate(owners)}
+    a, n = near.index(r), len(far)
+    order = [far[(a - i) % n] for i in range(n)]
+    return near, far, {c: order[i::len(owners)] for i, c in enumerate(owners)}
 
 
 def _pick(mask, k, avoid=0):
     bits = [b for b in range(mask.bit_length()) if (mask >> b) & 1 and not (avoid >> b) & 1]
     if len(bits) < k:
         bits = [b for b in range(mask.bit_length()) if (mask >> b) & 1]
-    return sum(1 << b for b in bits[:k])
+    return sum(1 << b for b in bits[::len(bits) // k][:k])
 
 
 def _common_mask(topo, src, dsts):
@@ -73,33 +80,6 @@ def _send(g, topo, src_ap, dst_ap, dsts, mask, remote_sem, local_sem):
                                           srcs=[src_ap], dsts=[dst_ap for _ in dsts])], local_sem=local_sem)
 
 
-def _tile(g, T, t, arrived, own, col):
-    S = T.sem
-    X, SQ, Z, R, D = T["x" + t], T["sq" + t], T["z" + t], T["r" + t], T["d" + t]
-    PZ, PS, PY = T["pz" + t], T["ps" + t], T["py" + t]
-    for q in (g.scalar, g.tensor):
-        for sem, v in arrived:
-            q.wait_ge(sem, v)
-    g.scalar.activation(SQ[:], X[:], ActivationFunctionType.Square).then_inc(S["sq" + t], 1)
-    g.tensor.matmul(PZ[:, 0:C], X[:], own, True, True).then_inc(S["pz" + t], 1)
-    g.tensor.wait_ge(S["sq" + t], 1)
-    g.tensor.matmul(PS[:, 0:1], SQ[:], T.one[:, 0:1], True, True).then_inc(S["ps" + t], 1)
-    g.vector.wait_ge(S["pz" + t], 1)
-    g.vector.tensor_copy(Z[:], PZ[:, 0:C]).then_inc(S["z" + t], 1)
-    g.vector.wait_ge(S["ps" + t], 1)
-    g.vector.reciprocal(R[:, 0:1], PS[:, 0:1]).then_inc(S["r" + t], 1)
-    g.scalar.wait_ge(S["r" + t], 1)
-    g.scalar.wait_ge(S.idm, 1)
-    g.scalar.activation(D[:], T.ident[:], ActivationFunctionType.Sqrt, scale=R[:, 0:1]).then_inc(S["d" + t], 1)
-    g.tensor.wait_ge(S["z" + t], 1)
-    g.tensor.wait_ge(S["d" + t], 1)
-    g.tensor.matmul(PY[0:C, 0:W], Z[:], D[:], True, True).then_inc(S["py" + t], 1)
-    g.vector.wait_ge(S["py" + t], 1)
-    g.vector.wait_ge(S.inv, 1)
-    g.vector.tensor_scalar(T.ysb[0:C, :, col, :], PY[0:C, 0:W], T.inv[0:C, 0:1], None,
-                           AluOpType.mult).then_inc(S["o" + t], 1)
-
-
 def _owner_program(g, core, T, topo):
     cores = list(T.cores)
     S = T.sem
@@ -109,12 +89,14 @@ def _owner_program(g, core, T, topo):
         near, far, jobs = _plan(T, topo, r)
         if core not in jobs:
             continue
-        slot = near.index(r)
+        cols = slice(near.index(r) * C, (near.index(r) + 1) * C)
         dsts = [cores[d] for d in jobs[core]]
         mask = _pick(_common_mask(topo, core, dsts), K_HOP2)
         g.wait_ge(S.rarr, K_HOP1)
-        _send(g, topo, T.rd[:], T.xb[:, slot * C:(slot + 1) * C], dsts, mask, S.arrb, S.snd)
-        g.wait_ge(S.snd, K_HOP2)
+        _send(g, topo, T.rd[:], T.xb[:, cols], dsts, mask, S.arrb, S.snd)
+        g.wait_ge(S.rarr2, K_INFO)
+        _send(g, topo, T.rd2[:], T.drb[:, cols], dsts, mask, S.arrd, S.snd)
+        g.wait_ge(S.snd, 2 * K_HOP2)
 
 
 def rank_program(g, core, T, topo):
@@ -126,16 +108,18 @@ def rank_program(g, core, T, topo):
     cores = list(T.cores)
     near, far, jobs = _plan(T, topo, r)
     assert near == list(range(near[0], N, 2)) and far == list(range(far[0], N, 2))
-    slot = near.index(r)
-    own = T.xa[:, slot * C:(slot + 1) * C]
+    cols = slice(near.index(r) * C, (near.index(r) + 1) * C)
+    own = T.xa[:, cols]
     peers = [cores[s] for s in near if s != r]
     owners = list(jobs)
+    sc, te, ve = g.scalar, g.tensor, g.vector
 
     g.sync.dma_start(T.xd[:], T.x[:]).then_inc(S.ldd, 16)
-    g.scalar.dma_start(own, T.x[:]).then_inc(S.ldx, 16)
+    sc.dma_start(own, T.x[:]).then_inc(S.ldx, 16)
 
-    g.vector.memset(T.onem[:], 1.0).then_inc(S.onem, 1)
-    g.vector.memset(T.one[:], 1.0).then_inc(S.one, 1)
+    ve.memset(T.onem[:], 1.0).then_inc(S.onem, 1)
+    ve.memset(T.sqf[:], 1.0).then_inc(S.sqm, 1)
+    ve.memset(T.one[:], 1.0).then_inc(S.one, 1)
     g.wait_ge(S.onem, 1)
     g.affine_select(T.ident[:], T.onem[:], [[-1, P]], AluOpType.is_equal, 0.0, 0, 1).then_inc(S.idm, 1)
 
@@ -145,21 +129,63 @@ def rank_program(g, core, T, topo):
     _send(g, topo, T.xd[:], T.rd[:], owners, m_hop1, S.rarr, S.snd)
     _send(g, topo, T.xd[:], own, peers, m_near, S.arra, S.snd)
 
-    g.scalar.wait_ge(S.ldx, 16)
-    g.scalar.activation(T.sqo[:], own, ActivationFunctionType.Square).then_inc(S.sqo, 1)
-    g.tensor.wait_ge(S.sqo, 1)
-    g.tensor.wait_ge(S.one, 1)
-    g.tensor.matmul(T.pso[0:C, 0:1], T.sqo[:], T.one[:, 0:1], True, True).then_inc(S.pso, 1)
-    g.vector.wait_ge(S.pso, 1)
-    g.vector.reciprocal(T.ro[0:C, 0:1], T.pso[0:C, 0:1]).then_inc(S.ro, 1)
-    g.scalar.wait_ge(S.ro, 1)
-    g.scalar.activation(T.inv[0:C, 0:1], T.ro[0:C, 0:1], ActivationFunctionType.Sqrt).then_inc(S.inv, 1)
+    sc.wait_ge(S.ldx, 16)
+    sc.wait_ge(S.sqm, 1)
+    sc.activation(T.sqf[:, cols], own, _ACT.Square).then_inc(S.sqo, 1)
+    te.wait_ge(S.sqm, 1)
+    te.wait_ge(S.sqo, 1)
+    te.wait_ge(S.one, 1)
+    te.matmul(T.psf[:, 0:1], T.sqf[:], T.one[:, 0:1], True, True).then_inc(S.psf, 1)
+    te.matmul(T.pso[0:C, 0:1], T.sqf[:, cols], T.one[:, 0:1], True, True).then_inc(S.pso, 1)
+    ve.wait_ge(S.psf, 1)
+    ve.reciprocal(T.rf[:, 0:1], T.psf[:, 0:1]).then_inc(S.rf, 1)
+    ve.wait_ge(S.rf, 1)
+    ve.wait_ge(S.idm, 1)
+    ve.tensor_scalar(T.drs[:], T.ident[:, cols], T.rf[:, 0:1], None, AluOpType.mult).then_inc(S.drs, 1)
+    g.wait_ge(S.drs, 1)
+    _send(g, topo, T.drs[:], T.rd2[:], owners, _pick(_common_mask(topo, core, owners), K_INFO), S.rarr2, S.snd)
+    ve.wait_ge(S.pso, 1)
+    ve.reciprocal(T.ro[0:C, 0:1], T.pso[0:C, 0:1]).then_inc(S.ro, 1)
+    sc.wait_ge(S.ro, 1)
+    sc.activation(T.inv[0:C, 0:1], T.ro[0:C, 0:1], _ACT.Sqrt).then_inc(S.inv, 1)
 
-    _tile(g, T, "a", [(S.ldx, 16), (S.arra, K_NEAR * len(peers))], own, near[0])
-    _tile(g, T, "b", [(S.arrb, K_HOP2 * len(far))], own, far[0])
+    for q in (sc, te):
+        q.wait_ge(S.ldx, 16)
+        q.wait_ge(S.arra, K_NEAR * len(peers))
+    sc.activation(T.sqa[:], T.xa[:], _ACT.Square).then_inc(S.sqa, 1)
+    te.matmul(T.pza[:, 0:C], T.xa[:], own, True, True).then_inc(S.pza, 1)
+    te.wait_ge(S.sqa, 1)
+    te.matmul(T.psa[:, 0:1], T.sqa[:], T.one[:, 0:1], True, True).then_inc(S.psa, 1)
+    ve.wait_ge(S.pza, 1)
+    ve.tensor_copy(T.za[:], T.pza[:, 0:C]).then_inc(S.za, 1)
+    ve.wait_ge(S.psa, 1)
+    ve.reciprocal(T.ra[:, 0:1], T.psa[:, 0:1]).then_inc(S.ra, 1)
+    sc.wait_ge(S.ra, 1)
+    sc.wait_ge(S.idm, 1)
+    sc.activation(T.da[:], T.ident[:], _ACT.Sqrt, scale=T.ra[:, 0:1]).then_inc(S.da, 1)
+    te.wait_ge(S.za, 1)
+    te.wait_ge(S.da, 1)
+    te.matmul(T.pya[0:C, 0:W], T.za[:], T.da[:], True, True).then_inc(S.pya, 1)
+    ve.wait_ge(S.pya, 1)
+    ve.wait_ge(S.inv, 1)
+    ve.tensor_scalar(T.ysb[0:C, :, near[0], :], T.pya[0:C, 0:W], T.inv[0:C, 0:1], None,
+                     AluOpType.mult).then_inc(S.oa, 1)
+
+    te.wait_ge(S.arrb, K_HOP2 * len(far))
+    te.matmul(T.pzb[:, 0:C], T.xb[:], own, True, True).then_inc(S.pzb, 1)
+    ve.wait_ge(S.pzb, 1)
+    ve.tensor_copy(T.zb[:], T.pzb[:, 0:C]).then_inc(S.zb, 1)
+    sc.wait_ge(S.arrd, K_HOP2 * len(far))
+    sc.activation(T.db[:], T.drb[:], _ACT.Sqrt).then_inc(S.db, 1)
+    te.wait_ge(S.zb, 1)
+    te.wait_ge(S.db, 1)
+    te.matmul(T.pyb[0:C, 0:W], T.zb[:], T.db[:], True, True).then_inc(S.pyb, 1)
+    ve.wait_ge(S.pyb, 1)
+    ve.tensor_scalar(T.ysb[0:C, :, far[0], :], T.pyb[0:C, 0:W], T.inv[0:C, 0:1], None,
+                     AluOpType.mult).then_inc(S.ob, 1)
 
     g.sync.wait_ge(S.oa, 1)
     g.sync.wait_ge(S.ob, 1)
     g.sync.dma_start(T.y[:], T.ysb[0:C]).then_inc(S.st, 16)
     g.sync.wait_ge(S.st, 16)
-    g.wait_ge(S.snd, K_HOP1 + K_NEAR)
+    g.wait_ge(S.snd, K_HOP1 + K_NEAR + K_INFO)

@@ -7,42 +7,30 @@ W = H * C
 K_HOP1 = 4
 K_HOP2 = 8
 K_NEAR = 8
-K_INFO = 16
+K_INFO = 8
 
 _BF, _F = "bfloat16", "float32"
 SCRATCH = {
     "xd": ("dram", [P, C], _BF),
     "rd": ("dram", [P, C], _BF),
     "rd2": ("dram", [P, C], _BF),
-    "xa": ("sbuf", [P, W], _BF),
+    "xa": ("sbuf", [P, H, 2 * C], _BF),
     "xb": ("sbuf", [P, W], _BF),
-    "drb": ("sbuf", [P, W], _BF),
-    "drs": ("sbuf", [P, C], _BF),
-    "sqf": ("sbuf", [P, W], _BF),
-    "sqa": ("sbuf", [P, W], _BF),
-    "one": ("sbuf", [P, 8], _BF),
-    "onem": ("sbuf", [P, P], _BF),
-    "ident": ("sbuf", [P, P], _BF),
-    "rf": ("sbuf", [P, 4], _F),
-    "ro": ("sbuf", [P, 4], _F),
-    "inv": ("sbuf", [P, 4], _F),
-    "ra": ("sbuf", [P, 4], _F),
-    "da": ("sbuf", [P, P], _BF),
-    "db": ("sbuf", [P, P], _BF),
-    "za": ("sbuf", [P, C], _BF),
-    "zb": ("sbuf", [P, C], _BF),
+    "rb": ("sbuf", [P, W], _BF),
+    "ones": ("sbuf", [P, P], _BF),
+    "sq": ("sbuf", [P, C], _BF),
+    "rr": ("sbuf", [P, C], _F),
+    "iv": ("sbuf", [P, C], _F),
+    "u": ("sbuf", [P, C], _BF),
+    "sa": ("sbuf", [P, H, C], _F),
+    "sb": ("sbuf", [P, W], _F),
     "ysb": ("sbuf", [P, H, 2, C], _BF),
-    "psf": ("psum", [P, 512], _F),
-    "pso": ("psum", [P, 512], _F),
+    "psn": ("psum", [P, 512], _F),
     "pza": ("psum", [P, 512], _F),
-    "psa": ("psum", [P, 512], _F),
-    "pya": ("psum", [P, 512], _F),
     "pzb": ("psum", [P, 512], _F),
-    "pyb": ("psum", [P, 512], _F),
 }
-SEMAPHORES = ["ldd", "ldx", "one", "onem", "sqm", "idm", "rarr", "rarr2", "arra", "arrb", "arrd", "snd", "st",
-              "sqo", "psf", "rf", "drs", "pso", "ro", "inv",
-              "sqa", "pza", "psa", "za", "ra", "da", "pya", "oa", "pzb", "zb", "db", "pyb", "ob"]
+SEMAPHORES = ["ldd", "ldx", "one", "rarr", "rarr2", "arra", "arrb", "arrd", "snd", "st",
+              "sq", "psn", "rr", "rrb", "iv", "u", "pza", "sa", "oa", "pzb", "sb", "ob"]
 _ACT = ActivationFunctionType
 
 
@@ -95,7 +83,7 @@ def _owner_program(g, core, T, topo):
         g.wait_ge(S.rarr, K_HOP1)
         _send(g, topo, T.rd[:], T.xb[:, cols], dsts, mask, S.arrb, S.snd)
         g.wait_ge(S.rarr2, K_INFO)
-        _send(g, topo, T.rd2[:], T.drb[:, cols], dsts, mask, S.arrd, S.snd)
+        _send(g, topo, T.rd2[:], T.rb[:, cols], dsts, mask, S.arrd, S.snd)
         g.wait_ge(S.snd, 2 * K_HOP2)
 
 
@@ -108,84 +96,67 @@ def rank_program(g, core, T, topo):
     cores = list(T.cores)
     near, far, jobs = _plan(T, topo, r)
     assert near == list(range(near[0], N, 2)) and far == list(range(far[0], N, 2))
-    cols = slice(near.index(r) * C, (near.index(r) + 1) * C)
-    own = T.xa[:, cols]
+    a = near.index(r)
+    own = T.xa[:, a, 0:C]
+    own_r = T.xa[:, a, C:2 * C]
     peers = [cores[s] for s in near if s != r]
     owners = list(jobs)
     sc, te, ve = g.scalar, g.tensor, g.vector
 
     g.sync.dma_start(T.xd[:], T.x[:]).then_inc(S.ldd, 16)
     sc.dma_start(own, T.x[:]).then_inc(S.ldx, 16)
-
-    ve.memset(T.onem[:], 1.0).then_inc(S.onem, 1)
-    ve.memset(T.sqf[:], 1.0).then_inc(S.sqm, 1)
-    ve.memset(T.one[:], 1.0).then_inc(S.one, 1)
-    g.wait_ge(S.onem, 1)
-    g.affine_select(T.ident[:], T.onem[:], [[-1, P]], AluOpType.is_equal, 0.0, 0, 1).then_inc(S.idm, 1)
+    ve.memset(T.ones[:], 1.0).then_inc(S.one, 1)
 
     m_near = _pick(_common_mask(topo, core, peers), K_NEAR)
     m_hop1 = _pick(_common_mask(topo, core, owners), K_HOP1, avoid=m_near)
+    m_info = _pick(_common_mask(topo, core, owners), K_INFO, avoid=m_near)
+
     g.wait_ge(S.ldd, 16)
     _send(g, topo, T.xd[:], T.rd[:], owners, m_hop1, S.rarr, S.snd)
-    _send(g, topo, T.xd[:], own, peers, m_near, S.arra, S.snd)
 
     sc.wait_ge(S.ldx, 16)
-    sc.wait_ge(S.sqm, 1)
-    sc.activation(T.sqf[:, cols], own, _ACT.Square).then_inc(S.sqo, 1)
-    te.wait_ge(S.sqm, 1)
-    te.wait_ge(S.sqo, 1)
+    sc.activation(T.sq[:], own, _ACT.Square).then_inc(S.sq, 1)
     te.wait_ge(S.one, 1)
-    te.matmul(T.psf[:, 0:1], T.sqf[:], T.one[:, 0:1], True, True).then_inc(S.psf, 1)
-    te.matmul(T.pso[0:C, 0:1], T.sqf[:, cols], T.one[:, 0:1], True, True).then_inc(S.pso, 1)
-    ve.wait_ge(S.psf, 1)
-    ve.reciprocal(T.rf[:, 0:1], T.psf[:, 0:1]).then_inc(S.rf, 1)
-    ve.wait_ge(S.rf, 1)
-    ve.wait_ge(S.idm, 1)
-    ve.tensor_scalar(T.drs[:], T.ident[:, cols], T.rf[:, 0:1], None, AluOpType.mult).then_inc(S.drs, 1)
-    g.wait_ge(S.drs, 1)
-    _send(g, topo, T.drs[:], T.rd2[:], owners, _pick(_common_mask(topo, core, owners), K_INFO), S.rarr2, S.snd)
-    ve.wait_ge(S.pso, 1)
-    ve.reciprocal(T.ro[0:C, 0:1], T.pso[0:C, 0:1]).then_inc(S.ro, 1)
-    sc.wait_ge(S.ro, 1)
-    sc.activation(T.inv[0:C, 0:1], T.ro[0:C, 0:1], _ACT.Sqrt).then_inc(S.inv, 1)
+    te.wait_ge(S.sq, 1)
+    te.matmul(T.psn[:, 0:C], T.ones[:], T.sq[:], True, True).then_inc(S.psn, 1)
+    ve.wait_ge(S.psn, 1)
+    ve.reciprocal(T.rr[:], T.psn[:, 0:C]).then_inc(S.rr, 1)
+    ve.wait_ge(S.rr, 1)
+    ve.tensor_copy(own_r, T.rr[:]).then_inc(S.rrb, 1)
 
-    for q in (sc, te):
-        q.wait_ge(S.ldx, 16)
-        q.wait_ge(S.arra, K_NEAR * len(peers))
-    sc.activation(T.sqa[:], T.xa[:], _ACT.Square).then_inc(S.sqa, 1)
-    te.matmul(T.pza[:, 0:C], T.xa[:], own, True, True).then_inc(S.pza, 1)
-    te.wait_ge(S.sqa, 1)
-    te.matmul(T.psa[:, 0:1], T.sqa[:], T.one[:, 0:1], True, True).then_inc(S.psa, 1)
-    ve.wait_ge(S.pza, 1)
-    ve.tensor_copy(T.za[:], T.pza[:, 0:C]).then_inc(S.za, 1)
-    ve.wait_ge(S.psa, 1)
-    ve.reciprocal(T.ra[:, 0:1], T.psa[:, 0:1]).then_inc(S.ra, 1)
-    sc.wait_ge(S.ra, 1)
-    sc.wait_ge(S.idm, 1)
-    sc.activation(T.da[:], T.ident[:], _ACT.Sqrt, scale=T.ra[:, 0:1]).then_inc(S.da, 1)
-    te.wait_ge(S.za, 1)
-    te.wait_ge(S.da, 1)
-    te.matmul(T.pya[0:C, 0:W], T.za[:], T.da[:], True, True).then_inc(S.pya, 1)
-    ve.wait_ge(S.pya, 1)
-    ve.wait_ge(S.inv, 1)
-    ve.tensor_scalar(T.ysb[0:C, :, near[0], :], T.pya[0:C, 0:W], T.inv[0:C, 0:1], None,
-                     AluOpType.mult).then_inc(S.oa, 1)
+    g.wait_ge(S.rrb, 1)
+    _send(g, topo, own_r, T.rd2[:], owners, m_info, S.rarr2, S.snd)
+    g.wait_ge(S.ldx, 16)
+    _send(g, topo, T.xa[:, a, :], T.xa[:, a, :], peers, m_near, S.arra, S.snd)
+
+    sc.wait_ge(S.rr, 1)
+    sc.activation(T.iv[:], T.rr[:], _ACT.Sqrt).then_inc(S.iv, 1)
+    ve.wait_ge(S.iv, 1)
+    ve.wait_ge(S.ldx, 16)
+    ve.tensor_tensor(T.u[:], own, T.iv[:], AluOpType.mult).then_inc(S.u, 1)
+
+    te.wait_ge(S.u, 1)
+    te.wait_ge(S.ldx, 16)
+    te.wait_ge(S.arra, K_NEAR * len(peers))
+    for k in range(H):
+        te.matmul(T.pza[0:C, k * C:(k + 1) * C], T.u[:], T.xa[:, k, 0:C], True, True).then_inc(S.pza, 1)
+    sc.wait_ge(S.rrb, 1)
+    sc.wait_ge(S.arra, K_NEAR * len(peers))
+    sc.activation(T.sa[0:C], T.xa[0:C, :, C:2 * C], _ACT.Sqrt).then_inc(S.sa, 1)
+    ve.wait_ge(S.pza, H)
+    ve.wait_ge(S.sa, 1)
+    ve.tensor_tensor(T.ysb[0:C, :, near[0], :], T.pza[0:C, 0:W], T.sa[0:C], AluOpType.mult).then_inc(S.oa, 1)
 
     te.wait_ge(S.arrb, K_HOP2 * len(far))
-    te.matmul(T.pzb[:, 0:C], T.xb[:], own, True, True).then_inc(S.pzb, 1)
-    ve.wait_ge(S.pzb, 1)
-    ve.tensor_copy(T.zb[:], T.pzb[:, 0:C]).then_inc(S.zb, 1)
+    te.matmul(T.pzb[0:C, 0:W], T.u[:], T.xb[:], True, True).then_inc(S.pzb, 1)
     sc.wait_ge(S.arrd, K_HOP2 * len(far))
-    sc.activation(T.db[:], T.drb[:], _ACT.Sqrt).then_inc(S.db, 1)
-    te.wait_ge(S.zb, 1)
-    te.wait_ge(S.db, 1)
-    te.matmul(T.pyb[0:C, 0:W], T.zb[:], T.db[:], True, True).then_inc(S.pyb, 1)
-    ve.wait_ge(S.pyb, 1)
-    ve.tensor_scalar(T.ysb[0:C, :, far[0], :], T.pyb[0:C, 0:W], T.inv[0:C, 0:1], None,
-                     AluOpType.mult).then_inc(S.ob, 1)
+    sc.activation(T.sb[0:C], T.rb[0:C], _ACT.Sqrt).then_inc(S.sb, 1)
+    ve.wait_ge(S.pzb, 1)
+    ve.wait_ge(S.sb, 1)
+    ve.tensor_tensor(T.ysb[0:C, :, far[0], :], T.pzb[0:C, 0:W], T.sb[0:C], AluOpType.mult).then_inc(S.ob, 1)
 
     g.sync.wait_ge(S.oa, 1)
     g.sync.wait_ge(S.ob, 1)
     g.sync.dma_start(T.y[:], T.ysb[0:C]).then_inc(S.st, 16)
     g.sync.wait_ge(S.st, 16)
-    g.wait_ge(S.snd, K_HOP1 + K_NEAR + K_INFO)
+    g.wait_ge(S.snd, K_HOP1 + K_INFO + K_NEAR)

from concourse.bass import DstId, RemoteDMATransfer
from concourse.mybir import AluOpType, ActivationFunctionType

P, N, C = 128, 8, 32
H = N // 2
W = H * C
K_HOP1 = 4
K_HOP2 = 8
K_NEAR = 8
K_INFO = 8

_BF, _F = "bfloat16", "float32"
SCRATCH = {
    "xd": ("dram", [P, C], _BF),
    "rd": ("dram", [P, C], _BF),
    "rd2": ("dram", [P, C], _BF),
    "xa": ("sbuf", [P, H, 2 * C], _BF),
    "xb": ("sbuf", [P, W], _BF),
    "rb": ("sbuf", [P, W], _BF),
    "ones": ("sbuf", [P, P], _BF),
    "sq": ("sbuf", [P, C], _BF),
    "rr": ("sbuf", [P, C], _F),
    "iv": ("sbuf", [P, C], _F),
    "u": ("sbuf", [P, C], _BF),
    "sa": ("sbuf", [P, H, C], _F),
    "sb": ("sbuf", [P, W], _F),
    "ysb": ("sbuf", [P, H, 2, C], _BF),
    "psn": ("psum", [P, 512], _F),
    "pza": ("psum", [P, 512], _F),
    "pzb": ("psum", [P, 512], _F),
}
SEMAPHORES = ["ldd", "ldx", "one", "rarr", "rarr2", "arra", "arrb", "arrd", "snd", "st",
              "sq", "psn", "rr", "rrb", "iv", "u", "pza", "sa", "oa", "pzb", "sb", "ob"]
_ACT = ActivationFunctionType


def _plan(T, topo, r):
    cores = list(T.cores)
    ch = topo.chip(cores[r])
    near = [s for s in range(len(cores))
            if topo.chip(cores[s]) == ch or topo.same_plane(topo.chip(cores[s]), ch)]
    far = [s for s in range(len(cores)) if s not in near]
    owners = [c for c in range(topo.CHIPS * topo.CORES_PER_CHIP)
              if topo.chip(c) == ch and c not in cores and all(topo.may_write(c, cores[d]) for d in far)]
    owners = owners[:len(far)]
    a, n = near.index(r), len(far)
    order = [far[(a - i) % n] for i in range(n)]
    return near, far, {c: order[i::len(owners)] for i, c in enumerate(owners)}


def _pick(mask, k, avoid=0):
    bits = [b for b in range(mask.bit_length()) if (mask >> b) & 1 and not (avoid >> b) & 1]
    if len(bits) < k:
        bits = [b for b in range(mask.bit_length()) if (mask >> b) & 1]
    return sum(1 << b for b in bits[::len(bits) // k][:k])


def _common_mask(topo, src, dsts):
    m = topo.mask(src, dsts[0])
    for d in dsts[1:]:
        m &= topo.mask(src, d)
    return m


def _send(g, topo, src_ap, dst_ap, dsts, mask, remote_sem, local_sem):
    ids = [DstId(rid=topo.addr(d)[0], pnc=topo.addr(d)[1]) for d in dsts]
    g.remote_dma_fused([RemoteDMATransfer(dst_ids=ids, dma_engine_mask=mask, remote_sem=remote_sem,
                                          srcs=[src_ap], dsts=[dst_ap for _ in dsts])], local_sem=local_sem)


def _owner_program(g, core, T, topo):
    cores = list(T.cores)
    S = T.sem
    for r in range(len(cores)):
        if topo.chip(cores[r]) != topo.chip(core):
            continue
        near, far, jobs = _plan(T, topo, r)
        if core not in jobs:
            continue
        cols = slice(near.index(r) * C, (near.index(r) + 1) * C)
        dsts = [cores[d] for d in jobs[core]]
        mask = _pick(_common_mask(topo, core, dsts), K_HOP2)
        g.wait_ge(S.rarr, K_HOP1)
        _send(g, topo, T.rd[:], T.xb[:, cols], dsts, mask, S.arrb, S.snd)
        g.wait_ge(S.rarr2, K_INFO)
        _send(g, topo, T.rd2[:], T.rb[:, cols], dsts, mask, S.arrd, S.snd)
        g.wait_ge(S.snd, 2 * K_HOP2)


def rank_program(g, core, T, topo):
    r = T.rank_of(core)
    if r is None:
        _owner_program(g, core, T, topo)
        return
    S = T.sem
    cores = list(T.cores)
    near, far, jobs = _plan(T, topo, r)
    assert near == list(range(near[0], N, 2)) and far == list(range(far[0], N, 2))
    a = near.index(r)
    own = T.xa[:, a, 0:C]
    own_r = T.xa[:, a, C:2 * C]
    peers = [cores[s] for s in near if s != r]
    owners = list(jobs)
    sc, te, ve = g.scalar, g.tensor, g.vector

    g.sync.dma_start(T.xd[:], T.x[:]).then_inc(S.ldd, 16)
    sc.dma_start(own, T.x[:]).then_inc(S.ldx, 16)
    ve.memset(T.ones[:], 1.0).then_inc(S.one, 1)

    m_near = _pick(_common_mask(topo, core, peers), K_NEAR)
    m_hop1 = _pick(_common_mask(topo, core, owners), K_HOP1, avoid=m_near)
    m_info = _pick(_common_mask(topo, core, owners), K_INFO, avoid=m_near)

    g.wait_ge(S.ldd, 16)
    _send(g, topo, T.xd[:], T.rd[:], owners, m_hop1, S.rarr, S.snd)

    sc.wait_ge(S.ldx, 16)
    sc.activation(T.sq[:], own, _ACT.Square).then_inc(S.sq, 1)
    te.wait_ge(S.one, 1)
    te.wait_ge(S.sq, 1)
    te.matmul(T.psn[:, 0:C], T.ones[:], T.sq[:], True, True).then_inc(S.psn, 1)
    ve.wait_ge(S.psn, 1)
    ve.reciprocal(T.rr[:], T.psn[:, 0:C]).then_inc(S.rr, 1)
    ve.wait_ge(S.rr, 1)
    ve.tensor_copy(own_r, T.rr[:]).then_inc(S.rrb, 1)

    g.wait_ge(S.rrb, 1)
    _send(g, topo, own_r, T.rd2[:], owners, m_info, S.rarr2, S.snd)
    g.wait_ge(S.ldx, 16)
    _send(g, topo, T.xa[:, a, :], T.xa[:, a, :], peers, m_near, S.arra, S.snd)

    sc.wait_ge(S.rr, 1)
    sc.activation(T.iv[:], T.rr[:], _ACT.Sqrt).then_inc(S.iv, 1)
    ve.wait_ge(S.iv, 1)
    ve.wait_ge(S.ldx, 16)
    ve.tensor_tensor(T.u[:], own, T.iv[:], AluOpType.mult).then_inc(S.u, 1)

    te.wait_ge(S.u, 1)
    te.wait_ge(S.ldx, 16)
    te.wait_ge(S.arra, K_NEAR * len(peers))
    for k in range(H):
        te.matmul(T.pza[0:C, k * C:(k + 1) * C], T.u[:], T.xa[:, k, 0:C], True, True).then_inc(S.pza, 1)
    sc.wait_ge(S.rrb, 1)
    sc.wait_ge(S.arra, K_NEAR * len(peers))
    sc.activation(T.sa[0:C], T.xa[0:C, :, C:2 * C], _ACT.Sqrt).then_inc(S.sa, 1)
    ve.wait_ge(S.pza, H)
    ve.wait_ge(S.sa, 1)
    ve.tensor_tensor(T.ysb[0:C, :, near[0], :], T.pza[0:C, 0:W], T.sa[0:C], AluOpType.mult).then_inc(S.oa, 1)

    te.wait_ge(S.arrb, K_HOP2 * len(far))
    te.matmul(T.pzb[0:C, 0:W], T.u[:], T.xb[:], True, True).then_inc(S.pzb, 1)
    sc.wait_ge(S.arrd, K_HOP2 * len(far))
    sc.activation(T.sb[0:C], T.rb[0:C], _ACT.Sqrt).then_inc(S.sb, 1)
    ve.wait_ge(S.pzb, 1)
    ve.wait_ge(S.sb, 1)
    ve.tensor_tensor(T.ysb[0:C, :, far[0], :], T.pzb[0:C, 0:W], T.sb[0:C], AluOpType.mult).then_inc(S.ob, 1)

    g.sync.wait_ge(S.oa, 1)
    g.sync.wait_ge(S.ob, 1)
    g.sync.dma_start(T.y[:], T.ysb[0:C]).then_inc(S.st, 16)
    g.sync.wait_ge(S.st, 16)
    g.wait_ge(S.snd, K_HOP1 + K_INFO + K_NEAR)
